import numpy as np
import ml_dtypes


def mxq(x, axis, fmt="e4m3"):
    dtype, down = {"e4m3": (ml_dtypes.float8_e4m3fn, 7), "e5m2": (ml_dtypes.float8_e5m2, 14)}[fmt]
    v = np.moveaxis(np.asarray(x, np.float32).astype(ml_dtypes.bfloat16).astype(np.float64), axis, -1)
    blocks = v.reshape(v.shape[:-1] + (-1, 32))
    amax = np.abs(blocks).max(-1, keepdims=True)
    byte = np.maximum(np.where(amax > 0, np.frexp(amax)[1] - 1 + 127, 0) - down, 1)
    scale = np.exp2(byte - 127.0)
    codes = (blocks / scale).astype(np.float32).astype(dtype).astype(np.float64)
    return np.moveaxis((codes * scale).reshape(v.shape), -1, axis)


WIDE = False


def mx_kscale(k):
    if not WIDE:
        return np.ones(k)
    levels = np.array([30, -30])
    if k % 512:
        return np.exp2(np.random.permutation(np.resize(levels, k // 32))).repeat(32)
    a = np.empty((k // 512, 16))
    for p in range(k // 512):
        a[p, :8] = np.random.permutation(np.resize(levels, 8))
        for g in range(8):
            far = levels[np.abs(levels - a[p, g]) >= 10]
            a[p, g + 8] = far[np.random.randint(len(far))]
    return np.exp2(a.ravel()).repeat(32)


def f64(x):
    return np.asarray(x).astype(np.float64)


def striped(idx):
    return np.tile(np.asarray(idx).reshape(-1, 16).T, (8, 1)).astype(np.uint16)


def unstriped(offs):
    return offs[:16].T.reshape(-1).astype(np.int64)


E2M1 = np.array([0.0, 0.5, 1.0, 1.5, 2.0, 3.0, 4.0, 6.0, -0.0, -0.5, -1.0, -1.5, -2.0, -3.0, -4.0, -6.0])


def pack_weight(w, fmt):
    k, n = w.shape
    w = f64(np.asarray(w, np.float32).astype(ml_dtypes.bfloat16)).reshape(k // 32, 32, n)
    amax = np.abs(w).max(1)
    if fmt == "e4m3":
        byte = np.frexp(amax)[1] - 1 + 127 - 7
    else:
        mant, ex = np.frexp(amax / 6.0)
        byte = np.where(mant > 0.5, ex, ex - 1) + 127
    byte = np.clip(np.where(amax > 0, byte, 1), 1, 254)
    scaled = (w * np.exp2(127.0 - byte)[:, None, :]).reshape(k, n).astype(np.float32)
    by_word = np.ascontiguousarray(scaled.reshape(k // 512, 128, 4, n).transpose(0, 1, 3, 2))
    if fmt == "e4m3":
        words = by_word.astype(ml_dtypes.float8_e4m3fn).view(np.uint8)
    else:
        c = by_word.astype(ml_dtypes.float4_e2m1fn).view(np.uint8) & 0xF
        words = (c[..., 0::2] | (c[..., 1::2] << 4)).reshape(k // 512, 128, 2 * n)
    return np.ascontiguousarray(words), np.ascontiguousarray(byte.astype(np.uint8).reshape(k // 512, 16, n))


def unpack_weight(words, scales, fmt):
    g, _, n = scales.shape
    words = np.ascontiguousarray(words).reshape(g, 128, n, -1)
    if fmt == "e4m3":
        vals = words.view(ml_dtypes.float8_e4m3fn).astype(np.float64)
    else:
        nib = np.empty((g, 128, n, 4), np.uint8)
        nib[..., 0::2] = words & 0xF
        nib[..., 1::2] = words >> 4
        vals = E2M1[nib]
    vals = vals * np.repeat(np.exp2(scales.astype(np.float64) - 127.0), 8, axis=1)[..., None]
    return vals.transpose(0, 1, 3, 2).reshape(g * 512, n)


K, T, J, R, C, N, E = 512, 2048, 256, 512, 512, 256, 128


def setup_inputs():
    n = np.random.standard_normal
    idx = np.random.permutation(T)[:J]
    idx2 = np.random.permutation(T)[:J]
    idx3 = np.random.permutation(C)[:J]
    idx4 = np.random.permutation(C)[:J]
    idx5 = np.random.permutation(J)[:E]
    idx6 = np.random.permutation(J)[:E]
    fk = mx_kscale(K)
    fr = mx_kscale(R)
    xtp = pack_weight(n((K, T)) / fk[:, None], "e2m1")
    wp = pack_weight(n((K, R)) * 1 / np.sqrt(K) * fk[:, None] * fr, "e4m3")
    wbp = pack_weight(n((R, N)) * 1 / np.sqrt(R) / fr[:, None], "e2m1")
    wsp = pack_weight(n((K, N)) * 1 / np.sqrt(K) * fk[:, None], "e4m3")
    return {
        "xt_words": xtp[0],
        "xt_scales": xtp[1],
        "w_words": wp[0],
        "w_scales": wp[1],
        "wb_words": wbp[0],
        "wb_scales": wbp[1],
        "ws_words": wsp[0],
        "ws_scales": wsp[1],
        "offs": striped(idx),
        "offs2": striped(idx2),
        "offs3": striped(idx3),
        "offs4": striped(idx4),
        "offs5": striped(idx5),
        "offs6": striped(idx6),
    }


def reference(xt_words, xt_scales, w_words, w_scales, wb_words, wb_scales, ws_words, ws_scales, offs, offs2, offs3, offs4, offs5, offs6):
    idx = unstriped(offs)
    idx2 = unstriped(offs2)
    idx3 = unstriped(offs3)
    idx4 = unstriped(offs4)
    idx5 = unstriped(offs5)
    idx6 = unstriped(offs6)
    xtu = unpack_weight(xt_words, xt_scales, "e2m1")
    wu = unpack_weight(w_words, w_scales, "e4m3")
    wbu = unpack_weight(wb_words, wb_scales, "e2m1")
    wsu = unpack_weight(ws_words, ws_scales, "e4m3")
    xtidxg = xtu[:, idx]
    a = wu.T @ xtidxg
    xtidx2g = xtu[:, idx2]
    b = wu.T @ xtidx2g
    pw = np.zeros((R, C))
    pw[:, idx3] = a
    hid = np.abs(pw[:, idx4] - b)
    hidq = mxq(hid, 0, "e5m2")
    p = wbu.T @ hidq + wsu.T @ xtidx2g
    y = np.maximum(p[:, idx5], p[:, idx6])
    return y

@@ -1,0 +1,176 @@
+from contextlib import ExitStack
+
+import concourse.mybir as mybir
+
+K, T, J, R, C, N, E = 512, 2048, 256, 512, 512, 256, 128
+FLOPS = 2 * K * R * J * 2 + 2 * R * N * J + 2 * K * N * J
+
+F32 = mybir.dt.float32
+BF16 = mybir.dt.bfloat16
+I32 = mybir.dt.int32
+U32 = mybir.dt.uint32
+U16 = mybir.dt.uint16
+U8 = mybir.dt.uint8
+E4M3 = mybir.dt.float8_e4m3fn_x4
+E5M2 = mybir.dt.float8_e5m2_x4
+E2M1 = mybir.dt.float4_e2m1fn_x4
+ALU = mybir.AluOpType
+ACT = mybir.ActivationFunctionType
+
+P = 128
+PACK = 4
+HALF = J // 2
+
+
+def tile_list_tied_board_skip_bestoftwo_kernel(
+    tc, xt_words, xt_scales, w_words, w_scales, wb_words, wb_scales, ws_words, ws_scales,
+    offs, offs2, offs3, offs4, offs5, offs6, out,
+):
+    nc = tc.nc
+    with ExitStack() as ctx:
+        sb = ctx.enter_context(tc.tile_pool(name="sb", bufs=1))
+        ps = ctx.enter_context(tc.psum_pool(name="ps", bufs=1))
+
+        def load_list(src, name):
+            t = sb.tile(list(src.shape), U16, name=name)
+            nc.sync.dma_start(t[:], src)
+            return t
+
+        def load_rows(queue, plane, src, q):
+            queue.dma_start(plane[32 * q : 32 * q + 4, :].bitcast(I32), src[0, 4 * q : 4 * q + 4, :].bitcast(I32))
+
+        xs = sb.tile([P, T], U8, name="xs")
+        wsc_raw = sb.tile([P, R], U8, name="wsc_raw")
+        ssc = sb.tile([P, N], U8, name="ssc", align_bytes=64)
+        bsc = sb.tile([P, N], U8, name="bsc", align_bytes=64)
+        xw = sb.tile([P, T], U16, name="xw")
+        w_raw = sb.tile([P, R], U32, name="w_raw")
+        sw = sb.tile([P, N], U32, name="sw", align_bytes=64)
+        bw = sb.tile([P, 2 * N], U8, name="bw", align_bytes=64)
+        boards = [sb.tile([P, C], F32, name="board%d" % t) for t in range(PACK)]
+        wp = sb.tile([P, R], U32, name="wp", align_bytes=64)
+        wsc = sb.tile([P, R], U8, name="wsc", align_bytes=64)
+        g1w = sb.tile([P, J], U16, name="g1w", align_bytes=64)
+        g1s = sb.tile([P, J], U8, name="g1s", align_bytes=64)
+        g2w = sb.tile([P, J], U16, name="g2w", align_bytes=64)
+        g2s = sb.tile([P, J], U8, name="g2s", align_bytes=64)
+
+        nc.vector.memset(xs[:].bitcast(I32), 0)
+        for plane in (wsc_raw, ssc, bsc):
+            nc.gpsimd.memset(plane[:].bitcast(I32), 0)
+        l1 = load_list(offs, "l1")
+        load_rows(nc.scalar, wsc_raw, w_scales, 0)
+        load_rows(nc.sync, wsc_raw, w_scales, 1)
+        load_rows(nc.scalar, xs, xt_scales, 0)
+        nc.sync.dma_start(xw[:].bitcast(I32), xt_words[0].bitcast(I32))
+        load_rows(nc.scalar, xs, xt_scales, 1)
+        nc.sync.dma_start(w_raw[:].bitcast(I32), w_words[0].rearrange("p n t -> p (n t)").bitcast(I32))
+        load_rows(nc.scalar, xs, xt_scales, 2)
+        load_rows(nc.sync, xs, xt_scales, 3)
+        load_rows(nc.sync, wsc_raw, w_scales, 2)
+        load_rows(nc.sync, wsc_raw, w_scales, 3)
+        l2 = load_list(offs2, "l2")
+        l3 = load_list(offs3, "l3")
+        l4 = load_list(offs4, "l4")
+        nc.sync.dma_start(sw[:].bitcast(I32), ws_words[0].rearrange("p n t -> p (n t)").bitcast(I32))
+        for q in range(4):
+            load_rows(nc.sync, ssc, ws_scales, q)
+        nc.sync.dma_start(bw[:].bitcast(I32), wb_words[0].bitcast(I32))
+        for q in range(4):
+            load_rows(nc.sync, bsc, wb_scales, q)
+        l5 = load_list(offs5, "l5")
+        l6 = load_list(offs6, "l6")
+        for t in range(PACK):
+            nc.vector.memset(boards[t][:], 0.0)
+
+        nc.scalar.copy(wp[:].rearrange("p (t c i) -> p c t i", t=4, i=4), w_raw[:].rearrange("p (c i t) -> p c t i", t=4, i=4))
+        nc.vector.tensor_copy(g1w[:], xw[:].indirect(l1[:]))
+        nc.vector.tensor_copy(g1s[:], xs[:].indirect(l1[:]))
+        nc.vector.tensor_copy(wsc[:].rearrange("p (t c i) -> p c t i", t=4, i=16), wsc_raw[:].rearrange("p (c i t) -> p c t i", t=4, i=16))
+
+        a_ps = [ps.tile([P, J], F32, name="a_ps%d" % t) for t in range(PACK)]
+        for t in range(PACK):
+            cols = slice(t * P, (t + 1) * P)
+            nc.tensor.matmul_mx(out=a_ps[t][:], lhsT=wp[:, cols].bitcast(E4M3), lhsT_scale=wsc[:, cols],
+                                rhs=g1w[:].bitcast(E2M1), rhs_scale=g1s[:], start=True, stop=True)
+        nc.vector.tensor_copy(g2w[:], xw[:].indirect(l2[:]))
+        nc.vector.tensor_copy(g2s[:], xs[:].indirect(l2[:]))
+        b_ps = [ps.tile([P, 2, J], F32, name="b_ps%d" % u) for u in range(2)]
+        for t in range(PACK):
+            cols = slice(t * P, (t + 1) * P)
+            nc.tensor.matmul_mx(out=b_ps[t // 2][:, t % 2, :], lhsT=wp[:, cols].bitcast(E4M3), lhsT_scale=wsc[:, cols],
+                                rhs=g2w[:].bitcast(E2M1), rhs_scale=g2s[:], start=True, stop=True)
+        p_ps = [ps.tile([P, J], F32, name="p_ps%d" % h) for h in range(2)]
+        for h in range(2):
+            cols = slice(h * P, (h + 1) * P)
+            nc.tensor.matmul_mx(out=p_ps[h][:], lhsT=sw[:, cols].bitcast(E4M3), lhsT_scale=ssc[:, cols],
+                                rhs=g2w[:].bitcast(E2M1), rhs_scale=g2s[:], start=True, stop=False)
+
+        a_sb = [sb.tile([P, J], F32, name="a_sb%d" % t) for t in range(PACK)]
+        picked = [sb.tile([P, 2, J], F32, name="picked%d" % u) for u in range(2)]
+        diff = [sb.tile([P, 2, J], F32, name="diff%d" % u) for u in range(2)]
+        hid = sb.tile([P, J, PACK], BF16, name="hid", align_bytes=64)
+        hq = sb.tile([P, J], U32, name="hq", align_bytes=64)
+        hs = sb.tile([P, J], U8, name="hs", align_bytes=64)
+
+        def vcopy(o, i):
+            nc.vector.tensor_copy(o, i)
+
+        def scopy(o, i):
+            nc.scalar.activation(o, i, ACT.Copy)
+
+        def leave(copy, t):
+            copy(a_sb[t][:], a_ps[t][:])
+
+        def place(copy, t):
+            copy(boards[t][:].indirect(l3[:]), a_sb[t][:])
+
+        def pick(copy, t, j0, j1):
+            copy(picked[t // 2][:, t % 2, j0:j1], boards[t][:].indirect(l4[:, j0 // 16 : j1 // 16]))
+
+        def subtract(u, j0, j1):
+            nc.vector.tensor_tensor(diff[u][:, :, j0:j1], picked[u][:, :, j0:j1], b_ps[u][:, :, j0:j1], ALU.subtract)
+
+        def magnitude(u, j0, j1):
+            nc.scalar.activation(hid[:, j0:j1, 2 * u : 2 * u + 2], diff[u][:, :, j0:j1].rearrange("p t j -> p j t"), ACT.Abs)
+
+        def quantise(j0, j1, last):
+            nc.vector.quantize_mx(out=hq[:, j0:j1].bitcast(E5M2), scales=hs[:, j0:j1], in_=hid[:, j0:j1, :].rearrange("p j t -> p (j t)"))
+            for h in range(2):
+                nc.tensor.matmul_mx(out=p_ps[h][:, j0:j1], lhsT=bw[:, 2 * h * P : 2 * (h + 1) * P].bitcast(E2M1),
+                                    lhsT_scale=bsc[:, h * P : (h + 1) * P],
+                                    rhs=hq[:, j0:j1].bitcast(E5M2), rhs_scale=hs[:, j0:j1], start=False, stop=last)
+
+        leave(scopy, 0)
+        leave(scopy, 1)
+        place(scopy, 0)
+        place(vcopy, 1)
+        leave(scopy, 2)
+        leave(scopy, 3)
+        pick(vcopy, 1, 0, J)
+        pick(vcopy, 0, 0, J)
+        place(scopy, 2)
+        subtract(0, 0, J)
+        place(vcopy, 3)
+        magnitude(0, 0, J)
+        pick(scopy, 2, 0, J)
+        pick(vcopy, 3, 0, HALF)
+        pick(scopy, 3, HALF, J)
+        subtract(1, 0, HALF)
+        subtract(1, HALF, J)
+        magnitude(1, 0, HALF)
+        magnitude(1, HALF, J)
+        quantise(0, HALF, False)
+        quantise(HALF, J, True)
+
+        p_sb = [sb.tile([P, J], F32, name="p_sb%d" % h) for h in range(2)]
+        first = sb.tile([P, 2, E], F32, name="first")
+        second = sb.tile([P, 2, E], F32, name="second")
+        best = sb.tile([P, 2, E], F32, name="best")
+        for h, copy in enumerate((vcopy, scopy)):
+            copy(p_sb[h][:], p_ps[h][:])
+            copy(first[:, h, :], p_sb[h][:].indirect(l5[:]))
+            copy(second[:, h, :], p_sb[h][:].indirect(l6[:]))
+        for h, queue in enumerate((nc.sync, nc.scalar)):
+            nc.vector.tensor_tensor(best[:, h, :], first[:, h, :], second[:, h, :], ALU.max)
+            queue.dma_start(out[h * P : (h + 1) * P, :], best[:, h, :])

@@ -40,7 +40,7 @@ def tile_list_tied_board_skip_bestoftwo_kernel(
             queue.dma_start(plane[32 * q : 32 * q + 4, :].bitcast(I32), src[0, 4 * q : 4 * q + 4, :].bitcast(I32))
 
         xs = sb.tile([P, T], U8, name="xs")
-        wsc_raw = sb.tile([P, R], U8, name="wsc_raw")
+        wsc_raw = sb.tile([P, R], U8, name="wsc_raw", tag="turn", align_bytes=64)
         ssc = sb.tile([P, N], U8, name="ssc", align_bytes=64)
         bsc = sb.tile([P, N], U8, name="bsc", align_bytes=64)
         xw = sb.tile([P, T], U16, name="xw")
@@ -52,24 +52,21 @@ def tile_list_tied_board_skip_bestoftwo_kernel(
         wsc = sb.tile([P, R], U8, name="wsc", align_bytes=64)
         g1w = sb.tile([P, J], U16, name="g1w", align_bytes=64)
         g1s = sb.tile([P, J], U8, name="g1s", align_bytes=64)
-        g2w = sb.tile([P, J], U16, name="g2w", align_bytes=64)
         g2s = sb.tile([P, J], U8, name="g2s", align_bytes=64)
 
         nc.vector.memset(xs[:].bitcast(I32), 0)
         for plane in (wsc_raw, ssc, bsc):
-            nc.gpsimd.memset(plane[:].bitcast(I32), 0)
+            nc.vector.memset(plane[:].bitcast(I32), 0)
         l1 = load_list(offs, "l1")
-        load_rows(nc.scalar, wsc_raw, w_scales, 0)
-        load_rows(nc.sync, wsc_raw, w_scales, 1)
-        load_rows(nc.scalar, xs, xt_scales, 0)
-        nc.sync.dma_start(xw[:].bitcast(I32), xt_words[0].bitcast(I32))
-        load_rows(nc.scalar, xs, xt_scales, 1)
-        nc.sync.dma_start(w_raw[:].bitcast(I32), w_words[0].rearrange("p n t -> p (n t)").bitcast(I32))
-        load_rows(nc.scalar, xs, xt_scales, 2)
-        load_rows(nc.sync, xs, xt_scales, 3)
-        load_rows(nc.sync, wsc_raw, w_scales, 2)
-        load_rows(nc.sync, wsc_raw, w_scales, 3)
+        nc.scalar.dma_start(w_raw[:].bitcast(I32), w_words[0].rearrange("p n t -> p (n t)").bitcast(I32))
         l2 = load_list(offs2, "l2")
+        load_rows(nc.scalar, xs, xt_scales, 0)
+        load_rows(nc.sync, xs, xt_scales, 2)
+        load_rows(nc.scalar, xs, xt_scales, 1)
+        load_rows(nc.sync, xs, xt_scales, 3)
+        nc.sync.dma_start(xw[:].bitcast(I32), xt_words[0].bitcast(I32))
+        for q in range(4):
+            load_rows(nc.sync, wsc_raw, w_scales, q)
         l3 = load_list(offs3, "l3")
         l4 = load_list(offs4, "l4")
         nc.sync.dma_start(sw[:].bitcast(I32), ws_words[0].rearrange("p n t -> p (n t)").bitcast(I32))
@@ -84,31 +81,31 @@ def tile_list_tied_board_skip_bestoftwo_kernel(
             nc.vector.memset(boards[t][:], 0.0)
 
         nc.scalar.copy(wp[:].rearrange("p (t c i) -> p c t i", t=4, i=4), w_raw[:].rearrange("p (c i t) -> p c t i", t=4, i=4))
-        nc.vector.tensor_copy(g1w[:], xw[:].indirect(l1[:]))
         nc.vector.tensor_copy(g1s[:], xs[:].indirect(l1[:]))
-        nc.vector.tensor_copy(wsc[:].rearrange("p (t c i) -> p c t i", t=4, i=16), wsc_raw[:].rearrange("p (c i t) -> p c t i", t=4, i=16))
+        nc.vector.tensor_copy(g2s[:], xs[:].indirect(l2[:]))
+        nc.vector.tensor_copy(g1w[:], xw[:].indirect(l1[:]))
+        for u in range(2):
+            nc.vector.tensor_copy(wsc[:].rearrange("p (t m) -> p t m", t=4)[:, 2 * u : 2 * u + 2, :],
+                                  wsc_raw[:].rearrange("p (m t) -> p t m", t=4)[:, 2 * u : 2 * u + 2, :])
 
-        a_ps = [ps.tile([P, J], F32, name="a_ps%d" % t) for t in range(PACK)]
+        a_ps = [ps.tile([P, J], F32, name="a_ps%d" % t, tag="bank%d" % t) for t in range(PACK)]
         for t in range(PACK):
             cols = slice(t * P, (t + 1) * P)
             nc.tensor.matmul_mx(out=a_ps[t][:], lhsT=wp[:, cols].bitcast(E4M3), lhsT_scale=wsc[:, cols],
                                 rhs=g1w[:].bitcast(E2M1), rhs_scale=g1s[:], start=True, stop=True)
+        g2w = sb.tile([P, J], U16, name="g2w", tag="turn", align_bytes=64)
         nc.vector.tensor_copy(g2w[:], xw[:].indirect(l2[:]))
-        nc.vector.tensor_copy(g2s[:], xs[:].indirect(l2[:]))
-        b_ps = [ps.tile([P, 2, J], F32, name="b_ps%d" % u) for u in range(2)]
-        for t in range(PACK):
-            cols = slice(t * P, (t + 1) * P)
-            nc.tensor.matmul_mx(out=b_ps[t // 2][:, t % 2, :], lhsT=wp[:, cols].bitcast(E4M3), lhsT_scale=wsc[:, cols],
-                                rhs=g2w[:].bitcast(E2M1), rhs_scale=g2s[:], start=True, stop=True)
-        p_ps = [ps.tile([P, J], F32, name="p_ps%d" % h) for h in range(2)]
-        for h in range(2):
-            cols = slice(h * P, (h + 1) * P)
-            nc.tensor.matmul_mx(out=p_ps[h][:], lhsT=sw[:, cols].bitcast(E4M3), lhsT_scale=ssc[:, cols],
-                                rhs=g2w[:].bitcast(E2M1), rhs_scale=g2s[:], start=True, stop=False)
+        b_ps = [ps.tile([P, PACK, HALF], F32, name="b_ps%d" % u, tag="bank%d" % (4 + u)) for u in range(2)]
+        for u in range(2):
+            for t in range(PACK):
+                cols = slice(t * P, (t + 1) * P)
+                nc.tensor.matmul_mx(out=b_ps[u][:, t, :], lhsT=wp[:, cols].bitcast(E4M3), lhsT_scale=wsc[:, cols],
+                                    rhs=g2w[:, u * HALF : (u + 1) * HALF].bitcast(E2M1), rhs_scale=g2s[:, u * HALF : (u + 1) * HALF],
+                                    start=True, stop=True)
 
         a_sb = [sb.tile([P, J], F32, name="a_sb%d" % t) for t in range(PACK)]
-        picked = [sb.tile([P, 2, J], F32, name="picked%d" % u) for u in range(2)]
-        diff = [sb.tile([P, 2, J], F32, name="diff%d" % u) for u in range(2)]
+        picked = [sb.tile([P, PACK, HALF], F32, name="picked%d" % u) for u in range(2)]
+        diff = [sb.tile([P, PACK, HALF], F32, name="diff%d" % u) for u in range(2)]
         hid = sb.tile([P, J, PACK], BF16, name="hid", align_bytes=64)
         hq = sb.tile([P, J], U32, name="hq", align_bytes=64)
         hs = sb.tile([P, J], U8, name="hs", align_bytes=64)
@@ -125,50 +122,67 @@ def tile_list_tied_board_skip_bestoftwo_kernel(
         def place(copy, t):
             copy(boards[t][:].indirect(l3[:]), a_sb[t][:])
 
-        def pick(copy, t, j0, j1):
-            copy(picked[t // 2][:, t % 2, j0:j1], boards[t][:].indirect(l4[:, j0 // 16 : j1 // 16]))
+        def pick(copy, t, u):
+            copy(picked[u][:, t, :], boards[t][:].indirect(l4[:, u * HALF // 16 : (u + 1) * HALF // 16]))
 
-        def subtract(u, j0, j1):
-            nc.vector.tensor_tensor(diff[u][:, :, j0:j1], picked[u][:, :, j0:j1], b_ps[u][:, :, j0:j1], ALU.subtract)
+        def subtract(u):
+            nc.vector.tensor_tensor(diff[u][:], picked[u][:], b_ps[u][:], ALU.subtract)
 
         def magnitude(u, j0, j1):
-            nc.scalar.activation(hid[:, j0:j1, 2 * u : 2 * u + 2], diff[u][:, :, j0:j1].rearrange("p t j -> p j t"), ACT.Abs)
+            nc.scalar.activation(hid[:, u * HALF + j0 : u * HALF + j1, :].rearrange("p (c i) t -> p c t i", i=4),
+                                 diff[u][:, :, j0:j1].rearrange("p t (c i) -> p c t i", i=4), ACT.Abs)
 
-        def quantise(j0, j1, last):
-            nc.vector.quantize_mx(out=hq[:, j0:j1].bitcast(E5M2), scales=hs[:, j0:j1], in_=hid[:, j0:j1, :].rearrange("p j t -> p (j t)"))
+        def magnitude_vector(u, j0, j1):
+            d = diff[u][:, :, j0:j1].rearrange("p t j -> p j t")
+            nc.vector.scalar_tensor_tensor(hid[:, u * HALF + j0 : u * HALF + j1, :], d, -1.0, d, ALU.mult, ALU.max)
+
+        def quantise(u):
+            js = slice(u * HALF, (u + 1) * HALF)
+            nc.vector.quantize_mx(out=hq[:, js].bitcast(E5M2), scales=hs[:, js], in_=hid[:, js, :].rearrange("p j t -> p (j t)"))
             for h in range(2):
-                nc.tensor.matmul_mx(out=p_ps[h][:, j0:j1], lhsT=bw[:, 2 * h * P : 2 * (h + 1) * P].bitcast(E2M1),
+                nc.tensor.matmul_mx(out=p_ps[h][u][:], lhsT=bw[:, 2 * h * P : 2 * (h + 1) * P].bitcast(E2M1),
                                     lhsT_scale=bsc[:, h * P : (h + 1) * P],
-                                    rhs=hq[:, j0:j1].bitcast(E5M2), rhs_scale=hs[:, j0:j1], start=False, stop=last)
+                                    rhs=hq[:, js].bitcast(E5M2), rhs_scale=hs[:, js], start=False, stop=True)
 
         leave(scopy, 0)
-        leave(scopy, 1)
+        leave(vcopy, 1)
+        leave(scopy, 2)
+        leave(vcopy, 3)
+        p_ps = [[ps.tile([P, HALF], F32, name="p_ps%d%d" % (h, u), tag="bank%d" % (6 + h if u else h)) for u in range(2)] for h in range(2)]
+        for u in range(2):
+            for h in range(2):
+                cols = slice(h * P, (h + 1) * P)
+                nc.tensor.matmul_mx(out=p_ps[h][u][:], lhsT=sw[:, cols].bitcast(E4M3), lhsT_scale=ssc[:, cols],
+                                    rhs=g2w[:, u * HALF : (u + 1) * HALF].bitcast(E2M1), rhs_scale=g2s[:, u * HALF : (u + 1) * HALF],
+                                    start=True, stop=False)
         place(scopy, 0)
         place(vcopy, 1)
-        leave(scopy, 2)
-        leave(scopy, 3)
-        pick(vcopy, 1, 0, J)
-        pick(vcopy, 0, 0, J)
         place(scopy, 2)
-        subtract(0, 0, J)
         place(vcopy, 3)
-        magnitude(0, 0, J)
-        pick(scopy, 2, 0, J)
-        pick(vcopy, 3, 0, HALF)
-        pick(scopy, 3, HALF, J)
-        subtract(1, 0, HALF)
-        subtract(1, HALF, J)
-        magnitude(1, 0, HALF)
-        magnitude(1, HALF, J)
-        quantise(0, HALF, False)
-        quantise(HALF, J, True)
+        pick(scopy, 0, 0)
+        pick(vcopy, 1, 0)
+        pick(scopy, 2, 0)
+        pick(vcopy, 3, 0)
+        pick(scopy, 0, 1)
+        pick(vcopy, 1, 1)
+        pick(scopy, 2, 1)
+        pick(scopy, 3, 1)
+        subtract(0)
+        subtract(1)
+        magnitude(0, 0, HALF)
+        magnitude(1, 0, HALF // 2)
+        magnitude_vector(1, HALF // 2, HALF)
+        quantise(0)
+        quantise(1)
 
         p_sb = [sb.tile([P, J], F32, name="p_sb%d" % h) for h in range(2)]
         first = sb.tile([P, 2, E], F32, name="first")
         second = sb.tile([P, 2, E], F32, name="second")
         best = sb.tile([P, 2, E], F32, name="best")
+        for h in range(2):
+            scopy(p_sb[h][:, :HALF], p_ps[h][0][:])
         for h, copy in enumerate((vcopy, scopy)):
-            copy(p_sb[h][:], p_ps[h][:])
+            copy(p_sb[h][:, HALF:], p_ps[h][1][:])
             copy(first[:, h, :], p_sb[h][:].indirect(l5[:]))
             copy(second[:, h, :], p_sb[h][:].indirect(l6[:]))
         for h, queue in enumerate((nc.sync, nc.scalar)):

from contextlib import ExitStack

import concourse.mybir as mybir

K, T, J, R, C, N, E = 512, 2048, 256, 512, 512, 256, 128
FLOPS = 2 * K * R * J * 2 + 2 * R * N * J + 2 * K * N * J

F32 = mybir.dt.float32
BF16 = mybir.dt.bfloat16
I32 = mybir.dt.int32
U32 = mybir.dt.uint32
U16 = mybir.dt.uint16
U8 = mybir.dt.uint8
E4M3 = mybir.dt.float8_e4m3fn_x4
E5M2 = mybir.dt.float8_e5m2_x4
E2M1 = mybir.dt.float4_e2m1fn_x4
ALU = mybir.AluOpType
ACT = mybir.ActivationFunctionType

P = 128
PACK = 4
HALF = J // 2


def tile_list_tied_board_skip_bestoftwo_kernel(
    tc, xt_words, xt_scales, w_words, w_scales, wb_words, wb_scales, ws_words, ws_scales,
    offs, offs2, offs3, offs4, offs5, offs6, out,
):
    nc = tc.nc
    with ExitStack() as ctx:
        sb = ctx.enter_context(tc.tile_pool(name="sb", bufs=1))
        ps = ctx.enter_context(tc.psum_pool(name="ps", bufs=1))

        def load_list(src, name):
            t = sb.tile(list(src.shape), U16, name=name)
            nc.sync.dma_start(t[:], src)
            return t

        def load_rows(queue, plane, src, q):
            queue.dma_start(plane[32 * q : 32 * q + 4, :].bitcast(I32), src[0, 4 * q : 4 * q + 4, :].bitcast(I32))

        xs = sb.tile([P, T], U8, name="xs")
        wsc_raw = sb.tile([P, R], U8, name="wsc_raw", tag="turn", align_bytes=64)
        ssc = sb.tile([P, N], U8, name="ssc", align_bytes=64)
        bsc = sb.tile([P, N], U8, name="bsc", align_bytes=64)
        xw = sb.tile([P, T], U16, name="xw")
        w_raw = sb.tile([P, R], U32, name="w_raw")
        sw = sb.tile([P, N], U32, name="sw", align_bytes=64)
        bw = sb.tile([P, 2 * N], U8, name="bw", align_bytes=64)
        boards = [sb.tile([P, C], F32, name="board%d" % t) for t in range(PACK)]
        wp = sb.tile([P, R], U32, name="wp", align_bytes=64)
        wsc = sb.tile([P, R], U8, name="wsc", align_bytes=64)
        g1w = sb.tile([P, J], U16, name="g1w", align_bytes=64)
        g1s = sb.tile([P, J], U8, name="g1s", align_bytes=64)
        g2s = sb.tile([P, J], U8, name="g2s", align_bytes=64)

        nc.vector.memset(xs[:].bitcast(I32), 0)
        for plane in (wsc_raw, ssc, bsc):
            nc.vector.memset(plane[:].bitcast(I32), 0)
        l1 = load_list(offs, "l1")
        nc.scalar.dma_start(w_raw[:].bitcast(I32), w_words[0].rearrange("p n t -> p (n t)").bitcast(I32))
        l2 = load_list(offs2, "l2")
        load_rows(nc.scalar, xs, xt_scales, 0)
        load_rows(nc.sync, xs, xt_scales, 2)
        load_rows(nc.scalar, xs, xt_scales, 1)
        load_rows(nc.sync, xs, xt_scales, 3)
        nc.sync.dma_start(xw[:].bitcast(I32), xt_words[0].bitcast(I32))
        for q in range(4):
            load_rows(nc.sync, wsc_raw, w_scales, q)
        l3 = load_list(offs3, "l3")
        l4 = load_list(offs4, "l4")
        nc.sync.dma_start(sw[:].bitcast(I32), ws_words[0].rearrange("p n t -> p (n t)").bitcast(I32))
        for q in range(4):
            load_rows(nc.sync, ssc, ws_scales, q)
        nc.sync.dma_start(bw[:].bitcast(I32), wb_words[0].bitcast(I32))
        for q in range(4):
            load_rows(nc.sync, bsc, wb_scales, q)
        l5 = load_list(offs5, "l5")
        l6 = load_list(offs6, "l6")
        for t in range(PACK):
            nc.vector.memset(boards[t][:], 0.0)

        nc.scalar.copy(wp[:].rearrange("p (t c i) -> p c t i", t=4, i=4), w_raw[:].rearrange("p (c i t) -> p c t i", t=4, i=4))
        nc.vector.tensor_copy(g1s[:], xs[:].indirect(l1[:]))
        nc.vector.tensor_copy(g2s[:], xs[:].indirect(l2[:]))
        nc.vector.tensor_copy(g1w[:], xw[:].indirect(l1[:]))
        for u in range(2):
            nc.vector.tensor_copy(wsc[:].rearrange("p (t m) -> p t m", t=4)[:, 2 * u : 2 * u + 2, :],
                                  wsc_raw[:].rearrange("p (m t) -> p t m", t=4)[:, 2 * u : 2 * u + 2, :])

        a_ps = [ps.tile([P, J], F32, name="a_ps%d" % t, tag="bank%d" % t) for t in range(PACK)]
        for t in range(PACK):
            cols = slice(t * P, (t + 1) * P)
            nc.tensor.matmul_mx(out=a_ps[t][:], lhsT=wp[:, cols].bitcast(E4M3), lhsT_scale=wsc[:, cols],
                                rhs=g1w[:].bitcast(E2M1), rhs_scale=g1s[:], start=True, stop=True)
        g2w = sb.tile([P, J], U16, name="g2w", tag="turn", align_bytes=64)
        nc.vector.tensor_copy(g2w[:], xw[:].indirect(l2[:]))
        b_ps = [ps.tile([P, PACK, HALF], F32, name="b_ps%d" % u, tag="bank%d" % (4 + u)) for u in range(2)]
        for u in range(2):
            for t in range(PACK):
                cols = slice(t * P, (t + 1) * P)
                nc.tensor.matmul_mx(out=b_ps[u][:, t, :], lhsT=wp[:, cols].bitcast(E4M3), lhsT_scale=wsc[:, cols],
                                    rhs=g2w[:, u * HALF : (u + 1) * HALF].bitcast(E2M1), rhs_scale=g2s[:, u * HALF : (u + 1) * HALF],
                                    start=True, stop=True)

        a_sb = [sb.tile([P, J], F32, name="a_sb%d" % t) for t in range(PACK)]
        picked = [sb.tile([P, PACK, HALF], F32, name="picked%d" % u) for u in range(2)]
        diff = [sb.tile([P, PACK, HALF], F32, name="diff%d" % u) for u in range(2)]
        hid = sb.tile([P, J, PACK], BF16, name="hid", align_bytes=64)
        hq = sb.tile([P, J], U32, name="hq", align_bytes=64)
        hs = sb.tile([P, J], U8, name="hs", align_bytes=64)

        def vcopy(o, i):
            nc.vector.tensor_copy(o, i)

        def scopy(o, i):
            nc.scalar.activation(o, i, ACT.Copy)

        def leave(copy, t):
            copy(a_sb[t][:], a_ps[t][:])

        def place(copy, t):
            copy(boards[t][:].indirect(l3[:]), a_sb[t][:])

        def pick(copy, t, u):
            copy(picked[u][:, t, :], boards[t][:].indirect(l4[:, u * HALF // 16 : (u + 1) * HALF // 16]))

        def subtract(u):
            nc.vector.tensor_tensor(diff[u][:], picked[u][:], b_ps[u][:], ALU.subtract)

        def magnitude(u, j0, j1):
            nc.scalar.activation(hid[:, u * HALF + j0 : u * HALF + j1, :].rearrange("p (c i) t -> p c t i", i=4),
                                 diff[u][:, :, j0:j1].rearrange("p t (c i) -> p c t i", i=4), ACT.Abs)

        def magnitude_vector(u, j0, j1):
            d = diff[u][:, :, j0:j1].rearrange("p t j -> p j t")
            nc.vector.scalar_tensor_tensor(hid[:, u * HALF + j0 : u * HALF + j1, :], d, -1.0, d, ALU.mult, ALU.max)

        def quantise(u):
            js = slice(u * HALF, (u + 1) * HALF)
            nc.vector.quantize_mx(out=hq[:, js].bitcast(E5M2), scales=hs[:, js], in_=hid[:, js, :].rearrange("p j t -> p (j t)"))
            for h in range(2):
                nc.tensor.matmul_mx(out=p_ps[h][u][:], lhsT=bw[:, 2 * h * P : 2 * (h + 1) * P].bitcast(E2M1),
                                    lhsT_scale=bsc[:, h * P : (h + 1) * P],
                                    rhs=hq[:, js].bitcast(E5M2), rhs_scale=hs[:, js], start=False, stop=True)

        leave(scopy, 0)
        leave(vcopy, 1)
        leave(scopy, 2)
        leave(vcopy, 3)
        p_ps = [[ps.tile([P, HALF], F32, name="p_ps%d%d" % (h, u), tag="bank%d" % (6 + h if u else h)) for u in range(2)] for h in range(2)]
        for u in range(2):
            for h in range(2):
                cols = slice(h * P, (h + 1) * P)
                nc.tensor.matmul_mx(out=p_ps[h][u][:], lhsT=sw[:, cols].bitcast(E4M3), lhsT_scale=ssc[:, cols],
                                    rhs=g2w[:, u * HALF : (u + 1) * HALF].bitcast(E2M1), rhs_scale=g2s[:, u * HALF : (u + 1) * HALF],
                                    start=True, stop=False)
        place(scopy, 0)
        place(vcopy, 1)
        place(scopy, 2)
        place(vcopy, 3)
        pick(scopy, 0, 0)
        pick(vcopy, 1, 0)
        pick(scopy, 2, 0)
        pick(vcopy, 3, 0)
        pick(scopy, 0, 1)
        pick(vcopy, 1, 1)
        pick(scopy, 2, 1)
        pick(scopy, 3, 1)
        subtract(0)
        subtract(1)
        magnitude(0, 0, HALF)
        magnitude(1, 0, HALF // 2)
        magnitude_vector(1, HALF // 2, HALF)
        quantise(0)
        quantise(1)

        p_sb = [sb.tile([P, J], F32, name="p_sb%d" % h) for h in range(2)]
        first = sb.tile([P, 2, E], F32, name="first")
        second = sb.tile([P, 2, E], F32, name="second")
        best = sb.tile([P, 2, E], F32, name="best")
        for h in range(2):
            scopy(p_sb[h][:, :HALF], p_ps[h][0][:])
        for h, copy in enumerate((vcopy, scopy)):
            copy(p_sb[h][:, HALF:], p_ps[h][1][:])
            copy(first[:, h, :], p_sb[h][:].indirect(l5[:]))
            copy(second[:, h, :], p_sb[h][:].indirect(l6[:]))
        for h, queue in enumerate((nc.sync, nc.scalar)):
            nc.vector.tensor_tensor(best[:, h, :], first[:, h, :], second[:, h, :], ALU.max)
            queue.dma_start(out[h * P : (h + 1) * P, :], best[:, h, :])
